import numpy as np
import ml_dtypes


def mxq(x, axis, fmt="e4m3"):
    dtype, down = {"e4m3": (ml_dtypes.float8_e4m3fn, 7), "e5m2": (ml_dtypes.float8_e5m2, 14)}[fmt]
    v = np.moveaxis(np.asarray(x, np.float32).astype(ml_dtypes.bfloat16).astype(np.float64), axis, -1)
    blocks = v.reshape(v.shape[:-1] + (-1, 32))
    amax = np.abs(blocks).max(-1, keepdims=True)
    byte = np.maximum(np.where(amax > 0, np.frexp(amax)[1] - 1 + 127, 0) - down, 1)
    scale = np.exp2(byte - 127.0)
    codes = (blocks / scale).astype(np.float32).astype(dtype).astype(np.float64)
    return np.moveaxis((codes * scale).reshape(v.shape), -1, axis)


WIDE = False


def mx_kscale(k):
    if not WIDE:
        return np.ones(k)
    levels = np.array([10, -10, 5, -5, 0])
    if k % 512:
        return np.exp2(np.random.permutation(np.resize(levels, k // 32))).repeat(32)
    a = np.empty((k // 512, 16))
    for p in range(k // 512):
        a[p, :8] = np.random.permutation(np.resize(levels, 8))
        for g in range(8):
            far = levels[np.abs(levels - a[p, g]) >= 10]
            a[p, g + 8] = far[np.random.randint(len(far))]
    return np.exp2(a.ravel()).repeat(32)


def f64(x):
    return np.asarray(x).astype(np.float64)


def striped(idx):
    return np.tile(np.asarray(idx).reshape(-1, 16).T, (8, 1)).astype(np.uint16)


def unstriped(offs):
    return offs[:16].T.reshape(-1).astype(np.int64)


E2M1 = np.array([0.0, 0.5, 1.0, 1.5, 2.0, 3.0, 4.0, 6.0, -0.0, -0.5, -1.0, -1.5, -2.0, -3.0, -4.0, -6.0])


def pack_weight(w, fmt):
    k, n = w.shape
    w = f64(np.asarray(w, np.float32).astype(ml_dtypes.bfloat16)).reshape(k // 32, 32, n)
    amax = np.abs(w).max(1)
    if fmt == "e4m3":
        byte = np.frexp(amax)[1] - 1 + 127 - 7
    else:
        mant, ex = np.frexp(amax / 6.0)
        byte = np.where(mant > 0.5, ex, ex - 1) + 127
    byte = np.clip(np.where(amax > 0, byte, 1), 1, 254)
    scaled = (w * np.exp2(127.0 - byte)[:, None, :]).reshape(k, n).astype(np.float32)
    by_word = np.ascontiguousarray(scaled.reshape(k // 512, 128, 4, n).transpose(0, 1, 3, 2))
    if fmt == "e4m3":
        words = by_word.astype(ml_dtypes.float8_e4m3fn).view(np.uint8)
    else:
        c = by_word.astype(ml_dtypes.float4_e2m1fn).view(np.uint8) & 0xF
        words = (c[..., 0::2] | (c[..., 1::2] << 4)).reshape(k // 512, 128, 2 * n)
    return np.ascontiguousarray(words), np.ascontiguousarray(byte.astype(np.uint8).reshape(k // 512, 16, n))


def unpack_weight(words, scales, fmt):
    g, _, n = scales.shape
    words = np.ascontiguousarray(words).reshape(g, 128, n, -1)
    if fmt == "e4m3":
        vals = words.view(ml_dtypes.float8_e4m3fn).astype(np.float64)
    else:
        nib = np.empty((g, 128, n, 4), np.uint8)
        nib[..., 0::2] = words & 0xF
        nib[..., 1::2] = words >> 4
        vals = E2M1[nib]
    vals = vals * np.repeat(np.exp2(scales.astype(np.float64) - 127.0), 8, axis=1)[..., None]
    return vals.transpose(0, 1, 3, 2).reshape(g * 512, n)


def bf(x):
    return np.asarray(x, np.float32).astype(ml_dtypes.bfloat16)


def planes(Y):
    r, m = Y.shape
    b = f64(bf(Y)).reshape(r // 32, 32, m)
    amax = np.abs(b).max(1)
    byte = np.clip(np.where(amax > 0, np.frexp(amax)[1] - 1 + 127 - 7, 1), 1, 254)
    codes = (b * np.exp2(127.0 - byte)[:, None, :]).reshape(r, m).astype(np.float32).astype(ml_dtypes.float8_e4m3fn).view(np.uint8)
    words = codes.reshape(r // 512, 128, 4, m).transpose(0, 1, 3, 2)
    return np.ascontiguousarray(words), np.ascontiguousarray(byte.astype(np.uint8).reshape(r // 512, 16, m))


D, T, I, U, Q, E = 512, 2048, 512, 1024, 256, 512


def setup_inputs():
    n = np.random.standard_normal
    idx = np.random.permutation(T)[:I]
    idx2 = np.random.permutation(U)[:Q]
    idx3 = np.random.permutation(U)[:Q]
    fd = mx_kscale(D)
    fi = mx_kscale(I)
    ti = np.ones(T)
    ti[idx] = fi
    keysp = pack_weight(n((D, T)) / fd[:, None], "e2m1")
    return {
        "queries": (n((D, U)) * 0.3 / np.sqrt(D) * fd[:, None]).astype(np.float32),
        "keys_words": keysp[0],
        "keys_scales": keysp[1],
        "size": (np.random.uniform(0.5, 2.0, (1, I)) * fi).astype(np.float32),
        "vals": (n((E, T)) / ti).astype(np.float32),
        "gate": (np.random.uniform(4.0, 12.0, (1, Q))).astype(np.float32),
        "stream": (n((E, U))).astype(np.float32),
        "offs": striped(idx),
        "offs2": striped(idx2),
        "offs3": striped(idx3),
    }


def reference(queries, keys_words, keys_scales, size, vals, gate, stream, offs, offs2, offs3):
    idx = unstriped(offs)
    idx2 = unstriped(offs2)
    idx3 = unstriped(offs3)
    keysu = unpack_weight(keys_words, keys_scales, "e2m1")
    queriesidx2q = mxq(f64(queries)[:, idx2], 0, "e4m3")
    keysidxg = keysu[:, idx]
    a = queriesidx2q.T @ keysidxg
    p = np.exp(a - np.max(a, axis=1, keepdims=True))
    w = p * f64(size) / np.sum(p, axis=1, keepdims=True)
    wt = w.T
    vt = f64(vals)[:, idx].T
    vtq = mxq(vt, 0, "e4m3")
    wtq = mxq(wt, 0, "e4m3")
    o = vtq.T @ wtq
    og = o * f64(gate)
    of = np.zeros((E, U))
    of[:, idx3] = og
    y = f64(stream) + of
    words, scales = planes(y)
    return y, words, scales

@@ -1,0 +1,220 @@
+from contextlib import ExitStack
+
+import concourse.mybir as mybir
+from concourse.masks import make_identity
+
+D, T, I, U, Q, E = 512, 2048, 512, 1024, 256, 512
+FLOPS = 2 * Q * I * D + 2 * E * Q * I
+
+F32 = mybir.dt.float32
+BF16 = mybir.dt.bfloat16
+I32 = mybir.dt.int32
+U32 = mybir.dt.uint32
+U16 = mybir.dt.uint16
+U8 = mybir.dt.uint8
+FP8X4 = mybir.dt.float8_e4m3fn_x4
+FP4X4 = mybir.dt.float4_e2m1fn_x4
+ALU = mybir.AluOpType
+ACT = mybir.ActivationFunctionType
+AX = mybir.AxisListType
+
+P = 128
+PACK = 4
+QT = Q // P
+NCH = 4
+CH = U // NCH
+
+
+def tile_attend_activerequests_pl_kernel(tc, queries, keys_words, keys_scales, size, vals, gate, stream,
+                                          offs, offs2, offs3, out_0, out_1, out_2):
+    nc = tc.nc
+    with ExitStack() as ctx:
+        sb = ctx.enter_context(tc.tile_pool(name="sb", bufs=1))
+        ps = ctx.enter_context(tc.psum_pool(name="ps", bufs=1))
+
+        slot_list = sb.tile([P, I // 16], U16, name="slot_list")
+        query_list = sb.tile([P, Q // 16], U16, name="query_list")
+        place_list = sb.tile([P, Q // 16], U16, name="place_list")
+        kw_pool = sb.tile([P, T], U16, name="kw_pool", align_bytes=64)
+        ks_pool = sb.tile([P, T], U8, name="ks_pool", align_bytes=64)
+        q_pool = [sb.tile([P, U], F32, name=f"q_pool{t}") for t in range(PACK)]
+        v_pool = [sb.tile([P, T], F32, name=f"v_pool{t}") for t in range(PACK)]
+        y = sb.tile([P, PACK, U], F32, name="y")
+        placed = [sb.tile([P, U], F32, name=f"placed{t}") for t in range(2)]
+        size_col = sb.tile([P, I // P], F32, name="size_col")
+        gate_col = sb.tile([P, Q // P], F32, name="gate_col")
+        ident = sb.tile([P, P], F32, name="ident")
+
+        nc.vector.memset(ks_pool[:].bitcast(I32), 0)
+        for t in range(2):
+            nc.vector.memset(placed[t][:].bitcast(I32), 0)
+        make_identity(nc, ident[:])
+
+        q_planes = queries.rearrange("(p t) u -> t p u", t=PACK)
+        v_planes = vals.rearrange("(p t) c -> t p c", t=PACK)
+        s_planes = stream.rearrange("(p t) u -> t p u", t=PACK)
+        y_planes = out_0.rearrange("(p t) u -> t p u", t=PACK)
+
+        nc.sync.dma_start(slot_list[:], offs)
+        nc.sync.dma_start(kw_pool[:].bitcast(I32), keys_words[0].bitcast(I32))
+        nc.sync.dma_start(query_list[:], offs2)
+        for k in range(4):
+            nc.scalar.dma_start(ks_pool[32 * k : 32 * k + 4, :].bitcast(I32),
+                                keys_scales[0, 4 * k : 4 * k + 4, :].bitcast(I32))
+        for t in range(PACK):
+            nc.sync.dma_start(q_pool[t][:], q_planes[t])
+        nc.scalar.dma_start(size_col[:], size.rearrange("o (p c) -> (o p) c", p=P))
+        nc.scalar.dma_start(gate_col[:], gate.rearrange("o (p c) -> (o p) c", p=P))
+        nc.sync.dma_start(v_pool[0][:], v_planes[0])
+        nc.sync.dma_start(v_pool[1][:], v_planes[1])
+        nc.sync.dma_start(place_list[:], offs3)
+        nc.sync.dma_start(v_pool[2][:], v_planes[2])
+        nc.sync.dma_start(v_pool[3][:], v_planes[3])
+        for t in range(PACK):
+            nc.sync.dma_start(y[:, t, :], s_planes[t])
+
+        def spread(col, n, tag):
+            bank = ps.tile([P, n, P], F32, name=tag + "_spread", tag=tag)
+            for c in range(n):
+                nc.tensor.transpose(bank[:, c, :], col[:, c : c + 1].to_broadcast([P, P]), ident[:])
+            row = sb.tile([P, P, n], F32, name=tag + "_row")
+            nc.scalar.copy(row[:], bank[:].rearrange("m c p -> m p c"))
+            return row[:].rearrange("m p c -> m (p c)")
+
+        size_row = spread(size_col, I // P, "turn_w0")
+        gate_row = spread(gate_col, Q // P, "turn_w1")
+
+        k_words = sb.tile([P, I], U16, name="k_words", align_bytes=64)
+        k_scales = sb.tile([P, I], U8, name="k_scales", align_bytes=64)
+        q_rows = sb.tile([P, Q, PACK], BF16, name="q_rows", align_bytes=64)
+        nc.vector.tensor_copy(k_words[:], kw_pool[:].indirect(slot_list[:]))
+        for t in range(PACK):
+            nc.vector.tensor_copy(q_rows[:, :, t], q_pool[t][:].indirect(query_list[:]))
+            if t == 1:
+                nc.vector.tensor_copy(k_scales[:], ks_pool[:].indirect(slot_list[:]))
+        q_codes = sb.tile([P, Q], U32, name="q_codes", align_bytes=64)
+        q_scales = sb.tile([P, Q], U8, name="q_scales", align_bytes=64)
+        nc.vector.quantize_mx(out=q_codes[:].bitcast(FP8X4), scales=q_scales[:],
+                              in_=q_rows[:].rearrange("p q t -> p (q t)"))
+
+        scores, neg_max, prob, total, inv_total, w_bf = [], [], [], [], [], []
+        for h in range(QT):
+            cols = slice(h * P, (h + 1) * P)
+            a = ps.tile([P, I], F32, name=f"scores{h}")
+            nc.tensor.matmul_mx(out=a[:], lhsT=q_codes[:, cols].bitcast(FP8X4), lhsT_scale=q_scales[:, cols],
+                                rhs=k_words[:].bitcast(FP4X4), rhs_scale=k_scales[:], start=True, stop=True)
+            scores.append(a)
+        for h in range(QT):
+            m = sb.tile([P, 1], F32, name=f"neg_max{h}")
+            nc.vector.tensor_reduce(out=m[:], in_=scores[h][:], axis=AX.X, op=ALU.max, negate=True)
+            e = sb.tile([P, I], F32, name=f"prob{h}")
+            s = sb.tile([P, 1], F32, name=f"total{h}")
+            nc.scalar.activation(out=e[:], in_=scores[h][:], func=ACT.Exp, bias=m[:], scale=1.0, accum_out=s[:])
+            prob.append(e)
+            total.append(s)
+
+        def turn(rows_bf, grouped_words, tag):
+            words = rows_bf[:].bitcast(F32)
+            bank = ps.tile([P, 2, P], F32, name=tag + "_bank", tag=tag)
+            for u in range(2):
+                nc.tensor.transpose(bank[:, u, :], words[:, u : 2 * P : 2], ident[:])
+            nc.scalar.copy(grouped_words, bank[:].rearrange("s u m -> s m u"))
+
+        v_rows = {}
+
+        def gather_values(t):
+            g = sb.tile([P, I], BF16, name=f"v_listed{t}", align_bytes=64)
+            nc.vector.tensor_copy(g[:], v_pool[t][:].indirect(slot_list[:]))
+            rows = sb.tile([P, P, PACK], BF16, name=f"v_rows{t}", align_bytes=64)
+            turn(g, rows[:].bitcast(F32), f"turn_v{t % 2}")
+            v_rows[t] = rows
+
+        gather_values(0)
+
+        w_rows = sb.tile([P, Q, PACK], BF16, name="w_rows", align_bytes=64)
+        for h in range(QT):
+            r = sb.tile([P, 1], F32, name=f"inv_total{h}")
+            nc.vector.reciprocal(r[:], total[h][:])
+            inv_total.append(r)
+        for h in range(QT):
+            w = sb.tile([P, I], BF16, name=f"w_bf{h}", align_bytes=64)
+            nc.vector.scalar_tensor_tensor(out=w[:], in0=prob[h][:], scalar=inv_total[h][:], in1=size_row,
+                                           op0=ALU.mult, op1=ALU.mult)
+            turn(w, w_rows[:, h * P : (h + 1) * P, :].bitcast(F32), f"turn_w{h}")
+
+        gather_values(1)
+
+        w_codes = sb.tile([P, Q], U32, name="w_codes", align_bytes=64)
+        w_scales = sb.tile([P, Q], U8, name="w_scales", align_bytes=64)
+        nc.vector.quantize_mx(out=w_codes[:].bitcast(FP8X4), scales=w_scales[:],
+                              in_=w_rows[:].rearrange("p q t -> p (q t)"))
+
+        o_sb = {}
+
+        def multiply(t):
+            codes = sb.tile([P, P], U32, name=f"v_codes{t}", align_bytes=64)
+            scales = sb.tile([P, P], U8, name=f"v_scales{t}", align_bytes=64)
+            nc.vector.quantize_mx(out=codes[:].bitcast(FP8X4), scales=scales[:],
+                                  in_=v_rows[t][:].rearrange("p m t -> p (m t)"))
+            bank = ps.tile([P, Q], F32, name=f"o_bank{t}", tag=f"o{t % 2}")
+            nc.tensor.matmul_mx(out=bank[:], lhsT=codes[:].bitcast(FP8X4), lhsT_scale=scales[:],
+                                rhs=w_codes[:].bitcast(FP8X4), rhs_scale=w_scales[:], start=True, stop=True)
+            o = sb.tile([P, Q], F32, name=f"o_sb{t}")
+            nc.scalar.copy(o[:], bank[:])
+            o_sb[t] = o
+
+        def scatter(t):
+            nc.vector.tensor_tensor(placed[t % 2][:].indirect(place_list[:]), o_sb[t][:], gate_row, ALU.mult)
+
+        def add_stream(t, cols):
+            nc.vector.tensor_tensor(y[:, t, cols], y[:, t, cols], placed[t % 2][:, cols], ALU.add)
+
+        whole = slice(0, U)
+        multiply(0)
+        gather_values(2)
+        multiply(1)
+        scatter(0)
+        gather_values(3)
+        multiply(2)
+        scatter(1)
+        add_stream(0, whole)
+        nc.sync.dma_start(y_planes[0], y[:, 0, :])
+        multiply(3)
+        scatter(2)
+        add_stream(1, whole)
+        nc.sync.dma_start(y_planes[1], y[:, 1, :])
+        scatter(3)
+        add_stream(2, whole)
+        nc.sync.dma_start(y_planes[2], y[:, 2, :])
+
+        y_codes = sb.tile([P, U], U32, name="y_codes", align_bytes=64)
+        y_scales = sb.tile([P, U], U8, name="y_scales", align_bytes=64)
+        y_rows = [sb.tile([P, CH, PACK], BF16, name=f"y_rows{c}", align_bytes=64) for c in range(NCH)]
+        chunk = [slice(c * CH, (c + 1) * CH) for c in range(NCH)]
+        words_out = out_1[0].rearrange("p c r -> p (c r)").bitcast(I32)
+
+        def regroup(c, copy):
+            copy(y_rows[c][:].rearrange("p (c i) t -> p c t i", i=4),
+                 y[:, :, chunk[c]].rearrange("p t (c i) -> p c t i", i=4))
+
+        def quantise(c):
+            nc.vector.quantize_mx(out=y_codes[:, chunk[c]].bitcast(FP8X4), scales=y_scales[:, chunk[c]],
+                                  in_=y_rows[c][:].rearrange("p c t -> p (c t)"))
+            nc.sync.dma_start(words_out[:, chunk[c]], y_codes[:, chunk[c]].bitcast(I32))
+
+        for c in range(NCH):
+            add_stream(3, chunk[c])
+            if c % 2 == 1:
+                half = slice((c - 1) * CH, (c + 1) * CH)
+                nc.sync.dma_start(y_planes[3][:, half], y[:, 3, half])
+        regroup(0, nc.scalar.copy)
+        regroup(1, nc.scalar.copy)
+        regroup(2, nc.vector.tensor_copy)
+        quantise(0)
+        regroup(3, nc.vector.tensor_copy)
+        quantise(2)
+        quantise(1)
+        quantise(3)
+        for k in range(4):
+            nc.scalar.dma_start(out_2[0, 4 * k : 4 * k + 4, :].bitcast(I32),
+                                y_scales[32 * k : 32 * k + 4, :].bitcast(I32))

@@ -38,7 +38,8 @@ def tile_attend_activerequests_pl_kernel(tc, queries, keys_words, keys_scales, s
         kw_pool = sb.tile([P, T], U16, name="kw_pool", align_bytes=64)
         ks_pool = sb.tile([P, T], U8, name="ks_pool", align_bytes=64)
         q_pool = [sb.tile([P, U], F32, name=f"q_pool{t}") for t in range(PACK)]
-        v_pool = [sb.tile([P, T], F32, name=f"v_pool{t}") for t in range(PACK)]
+        v_pool = [sb.tile([P, T], F32, name=f"v_pool{t}", tag=f"v_pool{t}", align_bytes=64) for t in range(PACK)]
+        s_pool = [sb.tile([P, U], F32, name=f"s_pool{t}", tag=f"s_pool{t}", align_bytes=64) for t in range(PACK)]
         y = sb.tile([P, PACK, U], F32, name="y")
         placed = [sb.tile([P, U], F32, name=f"placed{t}") for t in range(2)]
         size_col = sb.tile([P, I // P], F32, name="size_col")
@@ -55,8 +56,8 @@ def tile_attend_activerequests_pl_kernel(tc, queries, keys_words, keys_scales, s
         s_planes = stream.rearrange("(p t) u -> t p u", t=PACK)
         y_planes = out_0.rearrange("(p t) u -> t p u", t=PACK)
 
-        nc.sync.dma_start(slot_list[:], offs)
         nc.sync.dma_start(kw_pool[:].bitcast(I32), keys_words[0].bitcast(I32))
+        nc.sync.dma_start(slot_list[:], offs)
         nc.sync.dma_start(query_list[:], offs2)
         for k in range(4):
             nc.scalar.dma_start(ks_pool[32 * k : 32 * k + 4, :].bitcast(I32),
@@ -67,11 +68,11 @@ def tile_attend_activerequests_pl_kernel(tc, queries, keys_words, keys_scales, s
         nc.scalar.dma_start(gate_col[:], gate.rearrange("o (p c) -> (o p) c", p=P))
         nc.sync.dma_start(v_pool[0][:], v_planes[0])
         nc.sync.dma_start(v_pool[1][:], v_planes[1])
-        nc.sync.dma_start(place_list[:], offs3)
         nc.sync.dma_start(v_pool[2][:], v_planes[2])
         nc.sync.dma_start(v_pool[3][:], v_planes[3])
+        nc.sync.dma_start(place_list[:], offs3)
         for t in range(PACK):
-            nc.sync.dma_start(y[:, t, :], s_planes[t])
+            nc.sync.dma_start(s_pool[t][:], s_planes[t])
 
         def spread(col, n, tag):
             bank = ps.tile([P, n, P], F32, name=tag + "_spread", tag=tag)
@@ -88,27 +89,31 @@ def tile_attend_activerequests_pl_kernel(tc, queries, keys_words, keys_scales, s
         k_scales = sb.tile([P, I], U8, name="k_scales", align_bytes=64)
         q_rows = sb.tile([P, Q, PACK], BF16, name="q_rows", align_bytes=64)
         nc.vector.tensor_copy(k_words[:], kw_pool[:].indirect(slot_list[:]))
-        for t in range(PACK):
+        for t in range(PACK - 1):
             nc.vector.tensor_copy(q_rows[:, :, t], q_pool[t][:].indirect(query_list[:]))
             if t == 1:
                 nc.vector.tensor_copy(k_scales[:], ks_pool[:].indirect(slot_list[:]))
-        q_codes = sb.tile([P, Q], U32, name="q_codes", align_bytes=64)
+        q_codes = sb.tile([P, Q], U32, name="q_codes", tag="q_codes", align_bytes=64)
         q_scales = sb.tile([P, Q], U8, name="q_scales", align_bytes=64)
-        nc.vector.quantize_mx(out=q_codes[:].bitcast(FP8X4), scales=q_scales[:],
-                              in_=q_rows[:].rearrange("p q t -> p (q t)"))
+        for h in range(QT):
+            cols = slice(h * P, (h + 1) * P)
+            nc.vector.tensor_copy(q_rows[:, cols, PACK - 1],
+                                  q_pool[PACK - 1][:].indirect(query_list[:, h * P // 16 : (h + 1) * P // 16]))
+            nc.vector.quantize_mx(out=q_codes[:, cols].bitcast(FP8X4), scales=q_scales[:, cols],
+                                  in_=q_rows[:, cols, :].rearrange("p q t -> p (q t)"))
 
         scores, neg_max, prob, total, inv_total, w_bf = [], [], [], [], [], []
         for h in range(QT):
             cols = slice(h * P, (h + 1) * P)
-            a = ps.tile([P, I], F32, name=f"scores{h}")
+            a = ps.tile([P, I], F32, name=f"scores{h}", tag=f"scores{h}")
             nc.tensor.matmul_mx(out=a[:], lhsT=q_codes[:, cols].bitcast(FP8X4), lhsT_scale=q_scales[:, cols],
                                 rhs=k_words[:].bitcast(FP4X4), rhs_scale=k_scales[:], start=True, stop=True)
             scores.append(a)
         for h in range(QT):
-            m = sb.tile([P, 1], F32, name=f"neg_max{h}")
+            m = sb.tile([P, 1], F32, name=f"neg_max{h}", tag=f"neg_max{h}", align_bytes=64)
             nc.vector.tensor_reduce(out=m[:], in_=scores[h][:], axis=AX.X, op=ALU.max, negate=True)
-            e = sb.tile([P, I], F32, name=f"prob{h}")
-            s = sb.tile([P, 1], F32, name=f"total{h}")
+            e = sb.tile([P, I], F32, name=f"prob{h}", tag=f"prob{h}", align_bytes=64)
+            s = sb.tile([P, 1], F32, name=f"total{h}", tag=f"total{h}", align_bytes=64)
             nc.scalar.activation(out=e[:], in_=scores[h][:], func=ACT.Exp, bias=m[:], scale=1.0, accum_out=s[:])
             prob.append(e)
             total.append(s)
@@ -123,7 +128,7 @@ def tile_attend_activerequests_pl_kernel(tc, queries, keys_words, keys_scales, s
         v_rows = {}
 
         def gather_values(t):
-            g = sb.tile([P, I], BF16, name=f"v_listed{t}", align_bytes=64)
+            g = sb.tile([P, I], BF16, name=f"v_listed{t}", tag={0: "q_codes", 1: "total1", 2: "prob1"}.get(t, f"v_listed{t}"), align_bytes=64)
             nc.vector.tensor_copy(g[:], v_pool[t][:].indirect(slot_list[:]))
             rows = sb.tile([P, P, PACK], BF16, name=f"v_rows{t}", align_bytes=64)
             turn(g, rows[:].bitcast(F32), f"turn_v{t % 2}")
@@ -131,7 +136,7 @@ def tile_attend_activerequests_pl_kernel(tc, queries, keys_words, keys_scales, s
 
         gather_values(0)
 
-        w_rows = sb.tile([P, Q, PACK], BF16, name="w_rows", align_bytes=64)
+        w_rows = sb.tile([P, Q, PACK], BF16, name="w_rows", tag="w_rows", align_bytes=64)
         for h in range(QT):
             r = sb.tile([P, 1], F32, name=f"inv_total{h}")
             nc.vector.reciprocal(r[:], total[h][:])
@@ -143,43 +148,50 @@ def tile_attend_activerequests_pl_kernel(tc, queries, keys_words, keys_scales, s
             turn(w, w_rows[:, h * P : (h + 1) * P, :].bitcast(F32), f"turn_w{h}")
 
         gather_values(1)
+        gather_values(2)
 
         w_codes = sb.tile([P, Q], U32, name="w_codes", align_bytes=64)
         w_scales = sb.tile([P, Q], U8, name="w_scales", align_bytes=64)
         nc.vector.quantize_mx(out=w_codes[:].bitcast(FP8X4), scales=w_scales[:],
                               in_=w_rows[:].rearrange("p q t -> p (q t)"))
 
-        o_sb = {}
+        o_sb, o_bank = {}, {}
 
         def multiply(t):
-            codes = sb.tile([P, P], U32, name=f"v_codes{t}", align_bytes=64)
+            codes = sb.tile([P, P], U32, name=f"v_codes{t}", tag={1: "v_pool2", 2: "v_pool3"}.get(t, f"v_codes{t}"), align_bytes=64)
             scales = sb.tile([P, P], U8, name=f"v_scales{t}", align_bytes=64)
             nc.vector.quantize_mx(out=codes[:].bitcast(FP8X4), scales=scales[:],
                                   in_=v_rows[t][:].rearrange("p m t -> p (m t)"))
-            bank = ps.tile([P, Q], F32, name=f"o_bank{t}", tag=f"o{t % 2}")
+            bank = ps.tile([P, Q], F32, name=f"o_bank{t}", tag=("o0", "o1", "turn_v0", "turn_v1")[t])
             nc.tensor.matmul_mx(out=bank[:], lhsT=codes[:].bitcast(FP8X4), lhsT_scale=scales[:],
                                 rhs=w_codes[:].bitcast(FP8X4), rhs_scale=w_scales[:], start=True, stop=True)
-            o = sb.tile([P, Q], F32, name=f"o_sb{t}")
-            nc.scalar.copy(o[:], bank[:])
+            o_bank[t] = bank
+
+        def copy_out(t, o):
+            nc.scalar.copy(o, o_bank[t][:])
             o_sb[t] = o
 
         def scatter(t):
-            nc.vector.tensor_tensor(placed[t % 2][:].indirect(place_list[:]), o_sb[t][:], gate_row, ALU.mult)
+            nc.vector.tensor_tensor(placed[t % 2][:].indirect(place_list[:]), o_sb[t], gate_row, ALU.mult)
 
         def add_stream(t, cols):
-            nc.vector.tensor_tensor(y[:, t, cols], y[:, t, cols], placed[t % 2][:, cols], ALU.add)
+            nc.vector.tensor_tensor(y[:, t, cols], s_pool[t][:, cols], placed[t % 2][:, cols], ALU.add)
 
         whole = slice(0, U)
         multiply(0)
-        gather_values(2)
+        copy_out(0, sb.tile([P, Q], F32, name="o_first")[:])
         multiply(1)
-        scatter(0)
         gather_values(3)
+        o_next = sb.tile([P, 2, Q], F32, name="o_next", tag="v_listed3", align_bytes=64)
+        copy_out(1, o_next[:, 0, :])
+        scatter(0)
         multiply(2)
+        copy_out(2, o_next[:, 1, :])
+        multiply(3)
+        copy_out(3, sb.tile([P, Q], F32, name="o_last")[:])
         scatter(1)
         add_stream(0, whole)
         nc.sync.dma_start(y_planes[0], y[:, 0, :])
-        multiply(3)
         scatter(2)
         add_stream(1, whole)
         nc.sync.dma_start(y_planes[1], y[:, 1, :])

@@ -64,26 +64,22 @@ def tile_attend_activerequests_pl_kernel(tc, queries, keys_words, keys_scales, s
                                 keys_scales[0, 4 * k : 4 * k + 4, :].bitcast(I32))
         for t in range(PACK):
             nc.sync.dma_start(q_pool[t][:], q_planes[t])
-        nc.scalar.dma_start(size_col[:], size.rearrange("o (p c) -> (o p) c", p=P))
-        nc.scalar.dma_start(gate_col[:], gate.rearrange("o (p c) -> (o p) c", p=P))
         nc.sync.dma_start(v_pool[0][:], v_planes[0])
-        nc.sync.dma_start(v_pool[1][:], v_planes[1])
-        nc.sync.dma_start(v_pool[2][:], v_planes[2])
+        nc.sync.dma_start(size_col[:], size.rearrange("o (p c) -> (o p) c", p=P))
         nc.sync.dma_start(v_pool[3][:], v_planes[3])
+        nc.sync.dma_start(v_pool[1][:], v_planes[1])
+        nc.sync.dma_start(gate_col[:], gate.rearrange("o (p c) -> (o p) c", p=P))
+        nc.sync.dma_start(v_pool[2][:], v_planes[2])
+        nc.sync.dma_start(s_pool[0][:], s_planes[0])
         nc.sync.dma_start(place_list[:], offs3)
-        for t in range(PACK):
+        for t in range(1, PACK):
             nc.sync.dma_start(s_pool[t][:], s_planes[t])
 
         def spread(col, n, tag):
             bank = ps.tile([P, n, P], F32, name=tag + "_spread", tag=tag)
             for c in range(n):
                 nc.tensor.transpose(bank[:, c, :], col[:, c : c + 1].to_broadcast([P, P]), ident[:])
-            row = sb.tile([P, P, n], F32, name=tag + "_row")
-            nc.scalar.copy(row[:], bank[:].rearrange("m c p -> m p c"))
-            return row[:].rearrange("m p c -> m (p c)")
-
-        size_row = spread(size_col, I // P, "turn_w0")
-        gate_row = spread(gate_col, Q // P, "turn_w1")
+            return bank[:].rearrange("m c p -> m p c")
 
         k_words = sb.tile([P, I], U16, name="k_words", align_bytes=64)
         k_scales = sb.tile([P, I], U8, name="k_scales", align_bytes=64)
@@ -102,7 +98,8 @@ def tile_attend_activerequests_pl_kernel(tc, queries, keys_words, keys_scales, s
             nc.vector.quantize_mx(out=q_codes[:, cols].bitcast(FP8X4), scales=q_scales[:, cols],
                                   in_=q_rows[:, cols, :].rearrange("p q t -> p (q t)"))
 
-        scores, neg_max, prob, total, inv_total, w_bf = [], [], [], [], [], []
+        scores, prob = [], []
+        total = sb.tile([P, QT], F32, name="total", tag="total", align_bytes=64)
         for h in range(QT):
             cols = slice(h * P, (h + 1) * P)
             a = ps.tile([P, I], F32, name=f"scores{h}", tag=f"scores{h}")
@@ -113,10 +110,8 @@ def tile_attend_activerequests_pl_kernel(tc, queries, keys_words, keys_scales, s
             m = sb.tile([P, 1], F32, name=f"neg_max{h}", tag=f"neg_max{h}", align_bytes=64)
             nc.vector.tensor_reduce(out=m[:], in_=scores[h][:], axis=AX.X, op=ALU.max, negate=True)
             e = sb.tile([P, I], F32, name=f"prob{h}", tag=f"prob{h}", align_bytes=64)
-            s = sb.tile([P, 1], F32, name=f"total{h}", tag=f"total{h}", align_bytes=64)
-            nc.scalar.activation(out=e[:], in_=scores[h][:], func=ACT.Exp, bias=m[:], scale=1.0, accum_out=s[:])
+            nc.scalar.activation(out=e[:], in_=scores[h][:], func=ACT.Exp, bias=m[:], scale=1.0, accum_out=total[:, h : h + 1])
             prob.append(e)
-            total.append(s)
 
         def turn(rows_bf, grouped_words, tag):
             words = rows_bf[:].bitcast(F32)
@@ -128,22 +123,27 @@ def tile_attend_activerequests_pl_kernel(tc, queries, keys_words, keys_scales, s
         v_rows = {}
 
         def gather_values(t):
-            g = sb.tile([P, I], BF16, name=f"v_listed{t}", tag={0: "q_codes", 1: "total1", 2: "prob1"}.get(t, f"v_listed{t}"), align_bytes=64)
-            nc.vector.tensor_copy(g[:], v_pool[t][:].indirect(slot_list[:]))
-            rows = sb.tile([P, P, PACK], BF16, name=f"v_rows{t}", align_bytes=64)
+            g = sb.tile([P, I], BF16, name=f"v_listed{t}", tag={0: "q_codes", 3: "v_pool2"}.get(t, f"v_listed{t}"), align_bytes=64)
+            if t == 3:
+                nc.scalar.activation(g[:], v_last[:].indirect(slot_list[:]), ACT.Copy)
+            else:
+                nc.vector.tensor_copy(g[:], v_pool[t][:].indirect(slot_list[:]))
+            rows = sb.tile([P, P, PACK], BF16, name=f"v_rows{t}", tag={0: "v_pool3"}.get(t, f"v_rows{t}"), align_bytes=64)
             turn(g, rows[:].bitcast(F32), f"turn_v{t % 2}")
             v_rows[t] = rows
 
+        size_rows = spread(size_col, I // P, "o0")
+        v_last = sb.tile([P, T], BF16, name="v_last", align_bytes=64)
+        nc.scalar.activation(v_last[:], v_pool[3][:], ACT.Copy)
         gather_values(0)
 
         w_rows = sb.tile([P, Q, PACK], BF16, name="w_rows", tag="w_rows", align_bytes=64)
-        for h in range(QT):
-            r = sb.tile([P, 1], F32, name=f"inv_total{h}")
-            nc.vector.reciprocal(r[:], total[h][:])
-            inv_total.append(r)
+        inv_total = sb.tile([P, QT], F32, name="inv_total")
+        nc.vector.reciprocal(inv_total[:], total[:])
         for h in range(QT):
             w = sb.tile([P, I], BF16, name=f"w_bf{h}", align_bytes=64)
-            nc.vector.scalar_tensor_tensor(out=w[:], in0=prob[h][:], scalar=inv_total[h][:], in1=size_row,
+            nc.vector.scalar_tensor_tensor(out=w[:].rearrange("q (p c) -> q p c", p=P), in0=prob[h][:].rearrange("q (p c) -> q p c", p=P),
+                                           scalar=inv_total[:, h : h + 1], in1=size_rows,
                                            op0=ALU.mult, op1=ALU.mult)
             turn(w, w_rows[:, h * P : (h + 1) * P, :].bitcast(F32), f"turn_w{h}")
 
@@ -158,7 +158,7 @@ def tile_attend_activerequests_pl_kernel(tc, queries, keys_words, keys_scales, s
         o_sb, o_bank = {}, {}
 
         def multiply(t):
-            codes = sb.tile([P, P], U32, name=f"v_codes{t}", tag={1: "v_pool2", 2: "v_pool3"}.get(t, f"v_codes{t}"), align_bytes=64)
+            codes = sb.tile([P, P], U32, name=f"v_codes{t}", tag={1: "v_pool2", 2: "o_first"}.get(t, f"v_codes{t}"), align_bytes=64)
             scales = sb.tile([P, P], U8, name=f"v_scales{t}", align_bytes=64)
             nc.vector.quantize_mx(out=codes[:].bitcast(FP8X4), scales=scales[:],
                                   in_=v_rows[t][:].rearrange("p m t -> p (m t)"))
@@ -179,22 +179,24 @@ def tile_attend_activerequests_pl_kernel(tc, queries, keys_words, keys_scales, s
 
         whole = slice(0, U)
         multiply(0)
-        copy_out(0, sb.tile([P, Q], F32, name="o_first")[:])
+        copy_out(0, sb.tile([P, Q], F32, name="o_first", tag="o_first", align_bytes=64)[:])
+        gate_tile = sb.tile([P, P, Q // P], F32, name="gate_tile")
+        nc.scalar.copy(gate_tile[:], spread(gate_col, Q // P, "o1"))
+        gate_row = gate_tile[:].rearrange("m p c -> m (p c)")
         multiply(1)
+        copy_out(1, sb.tile([P, Q], F32, name="o_sb1")[:])
         gather_values(3)
-        o_next = sb.tile([P, 2, Q], F32, name="o_next", tag="v_listed3", align_bytes=64)
-        copy_out(1, o_next[:, 0, :])
         scatter(0)
-        multiply(2)
-        copy_out(2, o_next[:, 1, :])
-        multiply(3)
-        copy_out(3, sb.tile([P, Q], F32, name="o_last")[:])
         scatter(1)
+        multiply(2)
+        copy_out(2, sb.tile([P, Q], F32, name="o_sb2")[:])
         add_stream(0, whole)
         nc.sync.dma_start(y_planes[0], y[:, 0, :])
-        scatter(2)
+        multiply(3)
+        copy_out(3, sb.tile([P, Q], F32, name="o_sb3")[:])
         add_stream(1, whole)
         nc.sync.dma_start(y_planes[1], y[:, 1, :])
+        scatter(2)
         scatter(3)
         add_stream(2, whole)
         nc.sync.dma_start(y_planes[2], y[:, 2, :])
@@ -205,9 +207,13 @@ def tile_attend_activerequests_pl_kernel(tc, queries, keys_words, keys_scales, s
         chunk = [slice(c * CH, (c + 1) * CH) for c in range(NCH)]
         words_out = out_1[0].rearrange("p c r -> p (c r)").bitcast(I32)
 
-        def regroup(c, copy):
-            copy(y_rows[c][:].rearrange("p (c i) t -> p c t i", i=4),
-                 y[:, :, chunk[c]].rearrange("p t (c i) -> p c t i", i=4))
+        def regroup(c, pair, copy):
+            planes = slice(2 * pair, 2 * pair + 2)
+            copy(y_rows[c][:, :, planes].rearrange("p (c i) t -> p c t i", i=4),
+                 y[:, planes, chunk[c]].rearrange("p t (c i) -> p c t i", i=4))
+
+        for c in range(NCH):
+            regroup(c, 0, nc.scalar.copy)
 
         def quantise(c):
             nc.vector.quantize_mx(out=y_codes[:, chunk[c]].bitcast(FP8X4), scales=y_scales[:, chunk[c]],
@@ -219,14 +225,11 @@ def tile_attend_activerequests_pl_kernel(tc, queries, keys_words, keys_scales, s
             if c % 2 == 1:
                 half = slice((c - 1) * CH, (c + 1) * CH)
                 nc.sync.dma_start(y_planes[3][:, half], y[:, 3, half])
-        regroup(0, nc.scalar.copy)
-        regroup(1, nc.scalar.copy)
-        regroup(2, nc.vector.tensor_copy)
-        quantise(0)
-        regroup(3, nc.vector.tensor_copy)
-        quantise(2)
-        quantise(1)
-        quantise(3)
+        for c in range(NCH - 1):
+            regroup(c, 1, nc.scalar.copy)
+        regroup(NCH - 1, 1, nc.vector.tensor_copy)
+        for c in (0, 1, 3, 2):
+            quantise(c)
         for k in range(4):
             nc.scalar.dma_start(out_2[0, 4 * k : 4 * k + 4, :].bitcast(I32),
                                 y_scales[32 * k : 32 * k + 4, :].bitcast(I32))

@@ -218,18 +218,23 @@ def tile_attend_activerequests_pl_kernel(tc, queries, keys_words, keys_scales, s
         def quantise(c):
             nc.vector.quantize_mx(out=y_codes[:, chunk[c]].bitcast(FP8X4), scales=y_scales[:, chunk[c]],
                                   in_=y_rows[c][:].rearrange("p c t -> p (c t)"))
-            nc.sync.dma_start(words_out[:, chunk[c]], y_codes[:, chunk[c]].bitcast(I32))
 
         for c in range(NCH):
             add_stream(3, chunk[c])
             if c % 2 == 1:
                 half = slice((c - 1) * CH, (c + 1) * CH)
                 nc.sync.dma_start(y_planes[3][:, half], y[:, 3, half])
-        for c in range(NCH - 1):
-            regroup(c, 1, nc.scalar.copy)
-        regroup(NCH - 1, 1, nc.vector.tensor_copy)
-        for c in (0, 1, 3, 2):
+        regroup(0, 1, nc.scalar.copy)
+        regroup(1, 1, nc.scalar.copy)
+        regroup(2, 1, nc.vector.tensor_copy)
+        quantise(0)
+        regroup(3, 1, nc.vector.tensor_copy)
+        quantise(1)
+        nc.sync.dma_start(words_out[:, 0 : 2 * CH], y_codes[:, 0 : 2 * CH].bitcast(I32))
+        for c in (2, 3):
             quantise(c)
+            nc.sync.dma_start(words_out[:, chunk[c]], y_codes[:, chunk[c]].bitcast(I32))
         for k in range(4):
-            nc.scalar.dma_start(out_2[0, 4 * k : 4 * k + 4, :].bitcast(I32),
-                                y_scales[32 * k : 32 * k + 4, :].bitcast(I32))
+            queue = nc.scalar if k < 3 else nc.sync
+            queue.dma_start(out_2[0, 4 * k : 4 * k + 4, :].bitcast(I32),
+                            y_scales[32 * k : 32 * k + 4, :].bitcast(I32))

from contextlib import ExitStack

import concourse.mybir as mybir
from concourse.masks import make_identity

D, T, I, U, Q, E = 512, 2048, 512, 1024, 256, 512
FLOPS = 2 * Q * I * D + 2 * E * Q * I

F32 = mybir.dt.float32
BF16 = mybir.dt.bfloat16
I32 = mybir.dt.int32
U32 = mybir.dt.uint32
U16 = mybir.dt.uint16
U8 = mybir.dt.uint8
FP8X4 = mybir.dt.float8_e4m3fn_x4
FP4X4 = mybir.dt.float4_e2m1fn_x4
ALU = mybir.AluOpType
ACT = mybir.ActivationFunctionType
AX = mybir.AxisListType

P = 128
PACK = 4
QT = Q // P
NCH = 4
CH = U // NCH


def tile_attend_activerequests_pl_kernel(tc, queries, keys_words, keys_scales, size, vals, gate, stream,
                                          offs, offs2, offs3, out_0, out_1, out_2):
    nc = tc.nc
    with ExitStack() as ctx:
        sb = ctx.enter_context(tc.tile_pool(name="sb", bufs=1))
        ps = ctx.enter_context(tc.psum_pool(name="ps", bufs=1))

        slot_list = sb.tile([P, I // 16], U16, name="slot_list")
        query_list = sb.tile([P, Q // 16], U16, name="query_list")
        place_list = sb.tile([P, Q // 16], U16, name="place_list")
        kw_pool = sb.tile([P, T], U16, name="kw_pool", align_bytes=64)
        ks_pool = sb.tile([P, T], U8, name="ks_pool", align_bytes=64)
        q_pool = [sb.tile([P, U], F32, name=f"q_pool{t}") for t in range(PACK)]
        v_pool = [sb.tile([P, T], F32, name=f"v_pool{t}", tag=f"v_pool{t}", align_bytes=64) for t in range(PACK)]
        s_pool = [sb.tile([P, U], F32, name=f"s_pool{t}", tag=f"s_pool{t}", align_bytes=64) for t in range(PACK)]
        y = sb.tile([P, PACK, U], F32, name="y")
        placed = [sb.tile([P, U], F32, name=f"placed{t}") for t in range(2)]
        size_col = sb.tile([P, I // P], F32, name="size_col")
        gate_col = sb.tile([P, Q // P], F32, name="gate_col")
        ident = sb.tile([P, P], F32, name="ident")

        nc.vector.memset(ks_pool[:].bitcast(I32), 0)
        for t in range(2):
            nc.vector.memset(placed[t][:].bitcast(I32), 0)
        make_identity(nc, ident[:])

        q_planes = queries.rearrange("(p t) u -> t p u", t=PACK)
        v_planes = vals.rearrange("(p t) c -> t p c", t=PACK)
        s_planes = stream.rearrange("(p t) u -> t p u", t=PACK)
        y_planes = out_0.rearrange("(p t) u -> t p u", t=PACK)

        nc.sync.dma_start(kw_pool[:].bitcast(I32), keys_words[0].bitcast(I32))
        nc.sync.dma_start(slot_list[:], offs)
        nc.sync.dma_start(query_list[:], offs2)
        for k in range(4):
            nc.scalar.dma_start(ks_pool[32 * k : 32 * k + 4, :].bitcast(I32),
                                keys_scales[0, 4 * k : 4 * k + 4, :].bitcast(I32))
        for t in range(PACK):
            nc.sync.dma_start(q_pool[t][:], q_planes[t])
        nc.sync.dma_start(v_pool[0][:], v_planes[0])
        nc.sync.dma_start(size_col[:], size.rearrange("o (p c) -> (o p) c", p=P))
        nc.sync.dma_start(v_pool[3][:], v_planes[3])
        nc.sync.dma_start(v_pool[1][:], v_planes[1])
        nc.sync.dma_start(gate_col[:], gate.rearrange("o (p c) -> (o p) c", p=P))
        nc.sync.dma_start(v_pool[2][:], v_planes[2])
        nc.sync.dma_start(s_pool[0][:], s_planes[0])
        nc.sync.dma_start(place_list[:], offs3)
        for t in range(1, PACK):
            nc.sync.dma_start(s_pool[t][:], s_planes[t])

        def spread(col, n, tag):
            bank = ps.tile([P, n, P], F32, name=tag + "_spread", tag=tag)
            for c in range(n):
                nc.tensor.transpose(bank[:, c, :], col[:, c : c + 1].to_broadcast([P, P]), ident[:])
            return bank[:].rearrange("m c p -> m p c")

        k_words = sb.tile([P, I], U16, name="k_words", align_bytes=64)
        k_scales = sb.tile([P, I], U8, name="k_scales", align_bytes=64)
        q_rows = sb.tile([P, Q, PACK], BF16, name="q_rows", align_bytes=64)
        nc.vector.tensor_copy(k_words[:], kw_pool[:].indirect(slot_list[:]))
        for t in range(PACK - 1):
            nc.vector.tensor_copy(q_rows[:, :, t], q_pool[t][:].indirect(query_list[:]))
            if t == 1:
                nc.vector.tensor_copy(k_scales[:], ks_pool[:].indirect(slot_list[:]))
        q_codes = sb.tile([P, Q], U32, name="q_codes", tag="q_codes", align_bytes=64)
        q_scales = sb.tile([P, Q], U8, name="q_scales", align_bytes=64)
        for h in range(QT):
            cols = slice(h * P, (h + 1) * P)
            nc.vector.tensor_copy(q_rows[:, cols, PACK - 1],
                                  q_pool[PACK - 1][:].indirect(query_list[:, h * P // 16 : (h + 1) * P // 16]))
            nc.vector.quantize_mx(out=q_codes[:, cols].bitcast(FP8X4), scales=q_scales[:, cols],
                                  in_=q_rows[:, cols, :].rearrange("p q t -> p (q t)"))

        scores, prob = [], []
        total = sb.tile([P, QT], F32, name="total", tag="total", align_bytes=64)
        for h in range(QT):
            cols = slice(h * P, (h + 1) * P)
            a = ps.tile([P, I], F32, name=f"scores{h}", tag=f"scores{h}")
            nc.tensor.matmul_mx(out=a[:], lhsT=q_codes[:, cols].bitcast(FP8X4), lhsT_scale=q_scales[:, cols],
                                rhs=k_words[:].bitcast(FP4X4), rhs_scale=k_scales[:], start=True, stop=True)
            scores.append(a)
        for h in range(QT):
            m = sb.tile([P, 1], F32, name=f"neg_max{h}", tag=f"neg_max{h}", align_bytes=64)
            nc.vector.tensor_reduce(out=m[:], in_=scores[h][:], axis=AX.X, op=ALU.max, negate=True)
            e = sb.tile([P, I], F32, name=f"prob{h}", tag=f"prob{h}", align_bytes=64)
            nc.scalar.activation(out=e[:], in_=scores[h][:], func=ACT.Exp, bias=m[:], scale=1.0, accum_out=total[:, h : h + 1])
            prob.append(e)

        def turn(rows_bf, grouped_words, tag):
            words = rows_bf[:].bitcast(F32)
            bank = ps.tile([P, 2, P], F32, name=tag + "_bank", tag=tag)
            for u in range(2):
                nc.tensor.transpose(bank[:, u, :], words[:, u : 2 * P : 2], ident[:])
            nc.scalar.copy(grouped_words, bank[:].rearrange("s u m -> s m u"))

        v_rows = {}

        def gather_values(t):
            g = sb.tile([P, I], BF16, name=f"v_listed{t}", tag={0: "q_codes", 3: "v_pool2"}.get(t, f"v_listed{t}"), align_bytes=64)
            if t == 3:
                nc.scalar.activation(g[:], v_last[:].indirect(slot_list[:]), ACT.Copy)
            else:
                nc.vector.tensor_copy(g[:], v_pool[t][:].indirect(slot_list[:]))
            rows = sb.tile([P, P, PACK], BF16, name=f"v_rows{t}", tag={0: "v_pool3"}.get(t, f"v_rows{t}"), align_bytes=64)
            turn(g, rows[:].bitcast(F32), f"turn_v{t % 2}")
            v_rows[t] = rows

        size_rows = spread(size_col, I // P, "o0")
        v_last = sb.tile([P, T], BF16, name="v_last", align_bytes=64)
        nc.scalar.activation(v_last[:], v_pool[3][:], ACT.Copy)
        gather_values(0)

        w_rows = sb.tile([P, Q, PACK], BF16, name="w_rows", tag="w_rows", align_bytes=64)
        inv_total = sb.tile([P, QT], F32, name="inv_total")
        nc.vector.reciprocal(inv_total[:], total[:])
        for h in range(QT):
            w = sb.tile([P, I], BF16, name=f"w_bf{h}", align_bytes=64)
            nc.vector.scalar_tensor_tensor(out=w[:].rearrange("q (p c) -> q p c", p=P), in0=prob[h][:].rearrange("q (p c) -> q p c", p=P),
                                           scalar=inv_total[:, h : h + 1], in1=size_rows,
                                           op0=ALU.mult, op1=ALU.mult)
            turn(w, w_rows[:, h * P : (h + 1) * P, :].bitcast(F32), f"turn_w{h}")

        gather_values(1)
        gather_values(2)

        w_codes = sb.tile([P, Q], U32, name="w_codes", align_bytes=64)
        w_scales = sb.tile([P, Q], U8, name="w_scales", align_bytes=64)
        nc.vector.quantize_mx(out=w_codes[:].bitcast(FP8X4), scales=w_scales[:],
                              in_=w_rows[:].rearrange("p q t -> p (q t)"))

        o_sb, o_bank = {}, {}

        def multiply(t):
            codes = sb.tile([P, P], U32, name=f"v_codes{t}", tag={1: "v_pool2", 2: "o_first"}.get(t, f"v_codes{t}"), align_bytes=64)
            scales = sb.tile([P, P], U8, name=f"v_scales{t}", align_bytes=64)
            nc.vector.quantize_mx(out=codes[:].bitcast(FP8X4), scales=scales[:],
                                  in_=v_rows[t][:].rearrange("p m t -> p (m t)"))
            bank = ps.tile([P, Q], F32, name=f"o_bank{t}", tag=("o0", "o1", "turn_v0", "turn_v1")[t])
            nc.tensor.matmul_mx(out=bank[:], lhsT=codes[:].bitcast(FP8X4), lhsT_scale=scales[:],
                                rhs=w_codes[:].bitcast(FP8X4), rhs_scale=w_scales[:], start=True, stop=True)
            o_bank[t] = bank

        def copy_out(t, o):
            nc.scalar.copy(o, o_bank[t][:])
            o_sb[t] = o

        def scatter(t):
            nc.vector.tensor_tensor(placed[t % 2][:].indirect(place_list[:]), o_sb[t], gate_row, ALU.mult)

        def add_stream(t, cols):
            nc.vector.tensor_tensor(y[:, t, cols], s_pool[t][:, cols], placed[t % 2][:, cols], ALU.add)

        whole = slice(0, U)
        multiply(0)
        copy_out(0, sb.tile([P, Q], F32, name="o_first", tag="o_first", align_bytes=64)[:])
        gate_tile = sb.tile([P, P, Q // P], F32, name="gate_tile")
        nc.scalar.copy(gate_tile[:], spread(gate_col, Q // P, "o1"))
        gate_row = gate_tile[:].rearrange("m p c -> m (p c)")
        multiply(1)
        copy_out(1, sb.tile([P, Q], F32, name="o_sb1")[:])
        gather_values(3)
        scatter(0)
        scatter(1)
        multiply(2)
        copy_out(2, sb.tile([P, Q], F32, name="o_sb2")[:])
        add_stream(0, whole)
        nc.sync.dma_start(y_planes[0], y[:, 0, :])
        multiply(3)
        copy_out(3, sb.tile([P, Q], F32, name="o_sb3")[:])
        add_stream(1, whole)
        nc.sync.dma_start(y_planes[1], y[:, 1, :])
        scatter(2)
        scatter(3)
        add_stream(2, whole)
        nc.sync.dma_start(y_planes[2], y[:, 2, :])

        y_codes = sb.tile([P, U], U32, name="y_codes", align_bytes=64)
        y_scales = sb.tile([P, U], U8, name="y_scales", align_bytes=64)
        y_rows = [sb.tile([P, CH, PACK], BF16, name=f"y_rows{c}", align_bytes=64) for c in range(NCH)]
        chunk = [slice(c * CH, (c + 1) * CH) for c in range(NCH)]
        words_out = out_1[0].rearrange("p c r -> p (c r)").bitcast(I32)

        def regroup(c, pair, copy):
            planes = slice(2 * pair, 2 * pair + 2)
            copy(y_rows[c][:, :, planes].rearrange("p (c i) t -> p c t i", i=4),
                 y[:, planes, chunk[c]].rearrange("p t (c i) -> p c t i", i=4))

        for c in range(NCH):
            regroup(c, 0, nc.scalar.copy)

        def quantise(c):
            nc.vector.quantize_mx(out=y_codes[:, chunk[c]].bitcast(FP8X4), scales=y_scales[:, chunk[c]],
                                  in_=y_rows[c][:].rearrange("p c t -> p (c t)"))

        for c in range(NCH):
            add_stream(3, chunk[c])
            if c % 2 == 1:
                half = slice((c - 1) * CH, (c + 1) * CH)
                nc.sync.dma_start(y_planes[3][:, half], y[:, 3, half])
        regroup(0, 1, nc.scalar.copy)
        regroup(1, 1, nc.scalar.copy)
        regroup(2, 1, nc.vector.tensor_copy)
        quantise(0)
        regroup(3, 1, nc.vector.tensor_copy)
        quantise(1)
        nc.sync.dma_start(words_out[:, 0 : 2 * CH], y_codes[:, 0 : 2 * CH].bitcast(I32))
        for c in (2, 3):
            quantise(c)
            nc.sync.dma_start(words_out[:, chunk[c]], y_codes[:, chunk[c]].bitcast(I32))
        for k in range(4):
            queue = nc.scalar if k < 3 else nc.sync
            queue.dma_start(out_2[0, 4 * k : 4 * k + 4, :].bitcast(I32),
                            y_scales[32 * k : 32 * k + 4, :].bitcast(I32))
